import numpy as np
import ml_dtypes


def mxq(x, axis, fmt="e4m3"):
    dtype, down = {"e4m3": (ml_dtypes.float8_e4m3fn, 7), "e5m2": (ml_dtypes.float8_e5m2, 14)}[fmt]
    v = np.moveaxis(np.asarray(x, np.float32).astype(ml_dtypes.bfloat16).astype(np.float64), axis, -1)
    blocks = v.reshape(v.shape[:-1] + (-1, 32))
    amax = np.abs(blocks).max(-1, keepdims=True)
    byte = np.maximum(np.where(amax > 0, np.frexp(amax)[1] - 1 + 127, 0) - down, 1)
    scale = np.exp2(byte - 127.0)
    codes = (blocks / scale).astype(np.float32).astype(dtype).astype(np.float64)
    return np.moveaxis((codes * scale).reshape(v.shape), -1, axis)


WIDE = False


def mx_kscale(k):
    if not WIDE:
        return np.ones(k)
    levels = np.array([30, -30])
    if k % 512:
        return np.exp2(np.random.permutation(np.resize(levels, k // 32))).repeat(32)
    a = np.empty((k // 512, 16))
    for p in range(k // 512):
        a[p, :8] = np.random.permutation(np.resize(levels, 8))
        for g in range(8):
            far = levels[np.abs(levels - a[p, g]) >= 10]
            a[p, g + 8] = far[np.random.randint(len(far))]
    return np.exp2(a.ravel()).repeat(32)


def f64(x):
    return np.asarray(x).astype(np.float64)


def striped(idx):
    return np.tile(np.asarray(idx).reshape(-1, 16).T, (8, 1)).astype(np.uint16)


def unstriped(offs):
    return offs[:16].T.reshape(-1).astype(np.int64)


E2M1 = np.array([0.0, 0.5, 1.0, 1.5, 2.0, 3.0, 4.0, 6.0, -0.0, -0.5, -1.0, -1.5, -2.0, -3.0, -4.0, -6.0])


def pack_weight(w, fmt):
    k, n = w.shape
    w = f64(np.asarray(w, np.float32).astype(ml_dtypes.bfloat16)).reshape(k // 32, 32, n)
    amax = np.abs(w).max(1)
    if fmt in ("e4m3", "e5m2"):
        byte = np.frexp(amax)[1] - 1 + 127 - (7 if fmt == "e4m3" else 14)
    else:
        mant, ex = np.frexp(amax / 6.0)
        byte = np.where(mant > 0.5, ex, ex - 1) + 127
    byte = np.clip(np.where(amax > 0, byte, 1), 1, 254)
    scaled = (w * np.exp2(127.0 - byte)[:, None, :]).reshape(k, n).astype(np.float32)
    by_word = np.ascontiguousarray(scaled.reshape(k // 512, 128, 4, n).transpose(0, 1, 3, 2))
    if fmt in ("e4m3", "e5m2"):
        words = by_word.astype(ml_dtypes.float8_e4m3fn if fmt == "e4m3" else ml_dtypes.float8_e5m2).view(np.uint8)
    else:
        c = by_word.astype(ml_dtypes.float4_e2m1fn).view(np.uint8) & 0xF
        words = (c[..., 0::2] | (c[..., 1::2] << 4)).reshape(k // 512, 128, 2 * n)
    return np.ascontiguousarray(words), np.ascontiguousarray(byte.astype(np.uint8).reshape(k // 512, 16, n))


def unpack_weight(words, scales, fmt):
    g, _, n = scales.shape
    words = np.ascontiguousarray(words).reshape(g, 128, n, -1)
    if fmt in ("e4m3", "e5m2"):
        vals = words.view(ml_dtypes.float8_e4m3fn if fmt == "e4m3" else ml_dtypes.float8_e5m2).astype(np.float64)
    else:
        nib = np.empty((g, 128, n, 4), np.uint8)
        nib[..., 0::2] = words & 0xF
        nib[..., 1::2] = words >> 4
        vals = E2M1[nib]
    vals = vals * np.repeat(np.exp2(scales.astype(np.float64) - 127.0), 8, axis=1)[..., None]
    return vals.transpose(0, 1, 3, 2).reshape(g * 512, n)


def e4m3fn_bytes(y):
    return np.clip(np.asarray(y, np.float64), -448.0, 448.0).astype(np.float32).astype(ml_dtypes.float8_e4m3fn).view(np.uint8)


def e4m3fn_values(b):
    return np.asarray(b, np.uint8).view(ml_dtypes.float8_e4m3fn).astype(np.float64)


K, V, J, N = 512, 1024, 256, 256


def setup_inputs():
    n = np.random.standard_normal
    idx = np.random.permutation(V)[:J]
    fk = mx_kscale(K)
    wp = pack_weight(n((K, N)) * 1 / np.sqrt(K) / fk[:, None], "e2m1")
    w2p = pack_weight(n((K, N)) * 1 / np.sqrt(K) / fk[:, None], "e5m2")
    return {
        "ca": e4m3fn_bytes(60.0 * n((K, V))),
        "sa": (np.random.uniform(0.004, 0.012, (K, 1)) * fk[:, None]).astype(np.float32),
        "sb": (np.random.uniform(0.004, 0.012, (K, 1)) * fk[:, None]).astype(np.float32),
        "w_words": wp[0],
        "w_scales": wp[1],
        "w2_words": w2p[0],
        "w2_scales": w2p[1],
        "offs": striped(idx),
    }


def reference(ca, sa, sb, w_words, w_scales, w2_words, w2_scales, offs):
    idx = unstriped(offs)
    wu = unpack_weight(w_words, w_scales, "e2m1")
    w2u = unpack_weight(w2_words, w2_scales, "e5m2")
    z1 = np.maximum(e4m3fn_values(ca)[:, idx], 0.0) * f64(sa)
    z2 = np.maximum(-e4m3fn_values(ca)[:, idx], 0.0) * f64(sb)
    z1q = mxq(z1, 0, "e4m3")
    z2q = mxq(z2, 0, "e4m3")
    p = wu.T @ z1q + w2u.T @ z2q
    return p

@@ -1,0 +1,106 @@
+from contextlib import ExitStack
+
+import concourse.mybir as mybir
+
+K, V, J, N = 512, 1024, 256, 256
+FLOPS = 2 * 2 * K * N * J
+
+F32 = mybir.dt.float32
+BF16 = mybir.dt.bfloat16
+I32 = mybir.dt.int32
+U32 = mybir.dt.uint32
+U16 = mybir.dt.uint16
+U8 = mybir.dt.uint8
+FP8 = mybir.dt.float8_e4m3fn
+E4M3X4 = mybir.dt.float8_e4m3fn_x4
+E5M2X4 = mybir.dt.float8_e5m2_x4
+E2M1X4 = mybir.dt.float4_e2m1fn_x4
+ALU = mybir.AluOpType
+
+P = 128
+PACK = 4
+
+
+def tile_list_signedhalves_kernel(tc, ca, sa, sb, w_words, w_scales, w2_words, w2_scales, offs, out):
+    nc = tc.nc
+    with ExitStack() as ctx:
+        sbuf = ctx.enter_context(tc.tile_pool(name="sbuf", bufs=1))
+        psum = ctx.enter_context(tc.psum_pool(name="psum", bufs=1))
+
+        offsets = sbuf.tile([P, J // 16], U16, name="offsets")
+        table = [sbuf.tile([P, V], U8, name=f"table{t}") for t in range(PACK)]
+        w1 = sbuf.tile([P, 2 * N], U8, name="w1", align_bytes=64)
+        w2 = sbuf.tile([P, 4 * N], U8, name="w2", align_bytes=64)
+        w1_scale = sbuf.tile([P, N], U8, name="w1_scale", align_bytes=64)
+        w2_scale = sbuf.tile([P, N], U8, name="w2_scale", align_bytes=64)
+        rise = sbuf.tile([P, PACK], F32, name="rise")
+        fall = sbuf.tile([P, PACK], F32, name="fall")
+        neg_fall = sbuf.tile([P, PACK], F32, name="neg_fall")
+
+        nc.vector.memset(w1_scale[:].bitcast(I32), 0)
+        nc.vector.memset(w2_scale[:].bitcast(I32), 0)
+
+        ca_rows = ca.rearrange("(p t) v -> t p v", t=PACK)
+        nc.sync.dma_start(table[0][:], ca_rows[0])
+        nc.sync.dma_start(offsets[:], offs)
+        for t in range(1, PACK):
+            nc.sync.dma_start(table[t][:], ca_rows[t])
+        nc.gpsimd.dma_start(rise[:], sa.rearrange("(p t) o -> p (t o)", t=PACK))
+        nc.gpsimd.dma_start(fall[:], sb.rearrange("(p t) o -> p (t o)", t=PACK))
+        nc.sync.dma_start(w1[:].bitcast(I32), w_words[0].bitcast(I32))
+        nc.sync.dma_start(w2[:].bitcast(I32), w2_words[0].rearrange("p n r -> p (n r)").bitcast(I32))
+        for plane, rows in ((w1_scale, w_scales), (w2_scale, w2_scales)):
+            for q in range(4):
+                nc.sync.dma_start(plane[32 * q : 32 * q + 4, :].bitcast(I32), rows[0, 4 * q : 4 * q + 4, :].bitcast(I32))
+        nc.gpsimd.tensor_scalar(neg_fall[:], fall[:], -1.0, 0.0, ALU.mult, ALU.add)
+
+        picked = [sbuf.tile([P, J], U8, name=f"picked{t}") for t in range(PACK)]
+        level = [sbuf.tile([P, J], F32, name=f"level{t}") for t in range(PACK)]
+        for t in range(PACK):
+            nc.vector.tensor_copy(picked[t][:], table[t][:].indirect(offsets[:]))
+            nc.scalar.copy(level[t][:], picked[t][:].bitcast(FP8))
+
+        z1_rows = sbuf.tile([P, PACK, J], BF16, name="z1_rows")
+        z2_rows = sbuf.tile([P, PACK, J], BF16, name="z2_rows")
+        z1_in = sbuf.tile([P, J, PACK], BF16, name="z1_in", align_bytes=64)
+        z2_in = sbuf.tile([P, J, PACK], BF16, name="z2_in", align_bytes=64)
+        z1_codes = sbuf.tile([P, J], U32, name="z1_codes", align_bytes=64)
+        z2_codes = sbuf.tile([P, J], U32, name="z2_codes", align_bytes=64)
+        z1_scale = sbuf.tile([P, J], U8, name="z1_scale", align_bytes=64)
+        z2_scale = sbuf.tile([P, J], U8, name="z2_scale", align_bytes=64)
+
+        for t in range(PACK):
+            nc.vector.tensor_scalar(z1_rows[:, t, :], level[t][:], 0.0, rise[:, t : t + 1], ALU.max, ALU.mult)
+        nc.scalar.copy(z1_in[:], z1_rows[:].rearrange("p t j -> p j t"))
+        for t in range(PACK):
+            nc.vector.tensor_scalar(z2_rows[:, t, :], level[t][:], 0.0, neg_fall[:, t : t + 1], ALU.min, ALU.mult)
+        nc.vector.tensor_copy(z2_in[:], z2_rows[:].rearrange("p t j -> p j t"))
+        nc.vector.quantize_mx(z1_codes[:].bitcast(E4M3X4), z1_scale[:], z1_in[:].rearrange("p j t -> p (j t)"))
+        nc.vector.quantize_mx(z2_codes[:].bitcast(E4M3X4), z2_scale[:], z2_in[:].rearrange("p j t -> p (j t)"))
+
+        acc = [psum.tile([P, J], F32, name=f"acc{h}") for h in range(2)]
+        for h in range(2):
+            nc.tensor.matmul_mx(
+                acc[h][:],
+                lhsT=w1[:, 2 * P * h : 2 * P * (h + 1)].bitcast(E2M1X4),
+                lhsT_scale=w1_scale[:, P * h : P * (h + 1)],
+                rhs=z1_codes[:].bitcast(E4M3X4),
+                rhs_scale=z1_scale[:],
+                start=True,
+                stop=False,
+            )
+        for h in range(2):
+            nc.tensor.matmul_mx(
+                acc[h][:],
+                lhsT=w2[:, 4 * P * h : 4 * P * (h + 1)].bitcast(E5M2X4),
+                lhsT_scale=w2_scale[:, P * h : P * (h + 1)],
+                rhs=z2_codes[:].bitcast(E4M3X4),
+                rhs_scale=z2_scale[:],
+                start=False,
+                stop=True,
+            )
+        res = [sbuf.tile([P, J], F32, name=f"res{h}") for h in range(2)]
+        nc.scalar.copy(res[0][:], acc[0][:])
+        nc.scalar.dma_start(out[0:P, :], res[0][:])
+        nc.vector.tensor_copy(res[1][:], acc[1][:])
+        nc.sync.dma_start(out[P : 2 * P, :], res[1][:])

@@ -16,9 +16,13 @@ E4M3X4 = mybir.dt.float8_e4m3fn_x4
 E5M2X4 = mybir.dt.float8_e5m2_x4
 E2M1X4 = mybir.dt.float4_e2m1fn_x4
 ALU = mybir.AluOpType
+ACT = mybir.ActivationFunctionType
 
 P = 128
 PACK = 4
+HALF = J // 2
+RUN = 4
+SHARE = 64
 
 
 def tile_list_signedhalves_kernel(tc, ca, sa, sb, w_words, w_scales, w2_words, w2_scales, offs, out):
@@ -45,14 +49,14 @@ def tile_list_signedhalves_kernel(tc, ca, sa, sb, w_words, w_scales, w2_words, w
         nc.sync.dma_start(offsets[:], offs)
         for t in range(1, PACK):
             nc.sync.dma_start(table[t][:], ca_rows[t])
-        nc.gpsimd.dma_start(rise[:], sa.rearrange("(p t) o -> p (t o)", t=PACK))
-        nc.gpsimd.dma_start(fall[:], sb.rearrange("(p t) o -> p (t o)", t=PACK))
+        nc.sync.dma_start(rise[:], sa.rearrange("(p t) o -> p (t o)", t=PACK))
+        nc.sync.dma_start(fall[:], sb.rearrange("(p t) o -> p (t o)", t=PACK))
         nc.sync.dma_start(w1[:].bitcast(I32), w_words[0].bitcast(I32))
         nc.sync.dma_start(w2[:].bitcast(I32), w2_words[0].rearrange("p n r -> p (n r)").bitcast(I32))
         for plane, rows in ((w1_scale, w_scales), (w2_scale, w2_scales)):
             for q in range(4):
                 nc.sync.dma_start(plane[32 * q : 32 * q + 4, :].bitcast(I32), rows[0, 4 * q : 4 * q + 4, :].bitcast(I32))
-        nc.gpsimd.tensor_scalar(neg_fall[:], fall[:], -1.0, 0.0, ALU.mult, ALU.add)
+        nc.scalar.activation(neg_fall[:], fall[:], ACT.Copy, scale=-1.0)
 
         picked = [sbuf.tile([P, J], U8, name=f"picked{t}") for t in range(PACK)]
         level = [sbuf.tile([P, J], F32, name=f"level{t}") for t in range(PACK)]
@@ -60,47 +64,61 @@ def tile_list_signedhalves_kernel(tc, ca, sa, sb, w_words, w_scales, w2_words, w
             nc.vector.tensor_copy(picked[t][:], table[t][:].indirect(offsets[:]))
             nc.scalar.copy(level[t][:], picked[t][:].bitcast(FP8))
 
-        z1_rows = sbuf.tile([P, PACK, J], BF16, name="z1_rows")
-        z2_rows = sbuf.tile([P, PACK, J], BF16, name="z2_rows")
-        z1_in = sbuf.tile([P, J, PACK], BF16, name="z1_in", align_bytes=64)
-        z2_in = sbuf.tile([P, J, PACK], BF16, name="z2_in", align_bytes=64)
-        z1_codes = sbuf.tile([P, J], U32, name="z1_codes", align_bytes=64)
-        z2_codes = sbuf.tile([P, J], U32, name="z2_codes", align_bytes=64)
-        z1_scale = sbuf.tile([P, J], U8, name="z1_scale", align_bytes=64)
-        z2_scale = sbuf.tile([P, J], U8, name="z2_scale", align_bytes=64)
+        rows = [sbuf.tile([P, PACK, J], BF16, name=f"rows{z}") for z in range(2)]
+        woven = [[sbuf.tile([P, HALF, PACK], BF16, name=f"woven{z}{s}", align_bytes=64) for s in range(2)] for z in range(2)]
+        codes = [[sbuf.tile([P, HALF], U32, name=f"codes{z}{s}", align_bytes=64) for s in range(2)] for z in range(2)]
+        scales = [[sbuf.tile([P, HALF], U8, name=f"scales{z}{s}", align_bytes=64) for s in range(2)] for z in range(2)]
+        acc = [[psum.tile([P, HALF], F32, name=f"acc{s}{h}") for h in range(2)] for s in range(2)]
+        first = sbuf.tile([P, 2, HALF], F32, name="first")
+        last = [sbuf.tile([P, HALF], F32, name=f"last{h}") for h in range(2)]
+
+        def weave(copy, z, s, c0, c1):
+            copy(
+                woven[z][s][:, c0:c1, :].rearrange("p (c i) t -> p c t i", i=RUN),
+                rows[z][:, :, s * HALF + c0 : s * HALF + c1].rearrange("p t (c i) -> p c t i", i=RUN),
+            )
+
+        def quantize(z, s):
+            nc.vector.quantize_mx(codes[z][s][:].bitcast(E4M3X4), scales[z][s][:], woven[z][s][:].rearrange("p j t -> p (j t)"))
+
+        def multiply(z, s):
+            for h in range(2):
+                if z == 0:
+                    words, plane = w1[:, 2 * P * h : 2 * P * (h + 1)].bitcast(E2M1X4), w1_scale
+                else:
+                    words, plane = w2[:, 4 * P * h : 4 * P * (h + 1)].bitcast(E5M2X4), w2_scale
+                nc.tensor.matmul_mx(
+                    acc[s][h][:],
+                    lhsT=words,
+                    lhsT_scale=plane[:, P * h : P * (h + 1)],
+                    rhs=codes[z][s][:].bitcast(E4M3X4),
+                    rhs_scale=scales[z][s][:],
+                    start=(z == 0),
+                    stop=(z == 1),
+                )
 
         for t in range(PACK):
-            nc.vector.tensor_scalar(z1_rows[:, t, :], level[t][:], 0.0, rise[:, t : t + 1], ALU.max, ALU.mult)
-        nc.scalar.copy(z1_in[:], z1_rows[:].rearrange("p t j -> p j t"))
+            nc.vector.tensor_scalar(rows[0][:, t, :], level[t][:], 0.0, rise[:, t : t + 1], ALU.max, ALU.mult)
+        weave(nc.scalar.copy, 0, 0, 0, HALF)
+        weave(nc.scalar.copy, 0, 1, 0, HALF)
         for t in range(PACK):
-            nc.vector.tensor_scalar(z2_rows[:, t, :], level[t][:], 0.0, neg_fall[:, t : t + 1], ALU.min, ALU.mult)
-        nc.vector.tensor_copy(z2_in[:], z2_rows[:].rearrange("p t j -> p j t"))
-        nc.vector.quantize_mx(z1_codes[:].bitcast(E4M3X4), z1_scale[:], z1_in[:].rearrange("p j t -> p (j t)"))
-        nc.vector.quantize_mx(z2_codes[:].bitcast(E4M3X4), z2_scale[:], z2_in[:].rearrange("p j t -> p (j t)"))
-
-        acc = [psum.tile([P, J], F32, name=f"acc{h}") for h in range(2)]
+            nc.vector.tensor_scalar(rows[1][:, t, :], level[t][:], 0.0, neg_fall[:, t : t + 1], ALU.min, ALU.mult)
+        quantize(0, 0)
+        multiply(0, 0)
+        weave(nc.vector.tensor_copy, 1, 0, 0, HALF)
+        weave(nc.vector.tensor_copy, 1, 1, 0, HALF - SHARE)
+        weave(nc.scalar.copy, 1, 1, HALF - SHARE, HALF)
+        quantize(1, 0)
+        multiply(1, 0)
+        quantize(0, 1)
+        multiply(0, 1)
+        quantize(1, 1)
+        multiply(1, 1)
+        out_h = out.rearrange("(h p) j -> p h j", h=2)
         for h in range(2):
-            nc.tensor.matmul_mx(
-                acc[h][:],
-                lhsT=w1[:, 2 * P * h : 2 * P * (h + 1)].bitcast(E2M1X4),
-                lhsT_scale=w1_scale[:, P * h : P * (h + 1)],
-                rhs=z1_codes[:].bitcast(E4M3X4),
-                rhs_scale=z1_scale[:],
-                start=True,
-                stop=False,
-            )
-        for h in range(2):
-            nc.tensor.matmul_mx(
-                acc[h][:],
-                lhsT=w2[:, 4 * P * h : 4 * P * (h + 1)].bitcast(E5M2X4),
-                lhsT_scale=w2_scale[:, P * h : P * (h + 1)],
-                rhs=z2_codes[:].bitcast(E4M3X4),
-                rhs_scale=z2_scale[:],
-                start=False,
-                stop=True,
-            )
-        res = [sbuf.tile([P, J], F32, name=f"res{h}") for h in range(2)]
-        nc.scalar.copy(res[0][:], acc[0][:])
-        nc.scalar.dma_start(out[0:P, :], res[0][:])
-        nc.vector.tensor_copy(res[1][:], acc[1][:])
-        nc.sync.dma_start(out[P : 2 * P, :], res[1][:])
+            nc.scalar.copy(first[:, h, :], acc[0][h][:])
+        nc.sync.dma_start(out_h[:, :, 0:HALF], first[:])
+        nc.scalar.copy(last[0][:], acc[1][0][:])
+        nc.scalar.dma_start(out[0:P, HALF:J], last[0][:])
+        nc.vector.tensor_copy(last[1][:], acc[1][1][:])
+        nc.sync.dma_start(out[P : 2 * P, HALF:J], last[1][:])

@@ -22,7 +22,6 @@ P = 128
 PACK = 4
 HALF = J // 2
 RUN = 4
-SHARE = 64
 
 
 def tile_list_signedhalves_kernel(tc, ca, sa, sb, w_words, w_scales, w2_words, w2_scales, offs, out):
@@ -51,8 +50,8 @@ def tile_list_signedhalves_kernel(tc, ca, sa, sb, w_words, w_scales, w2_words, w
             nc.sync.dma_start(table[t][:], ca_rows[t])
         nc.sync.dma_start(rise[:], sa.rearrange("(p t) o -> p (t o)", t=PACK))
         nc.sync.dma_start(fall[:], sb.rearrange("(p t) o -> p (t o)", t=PACK))
-        nc.sync.dma_start(w1[:].bitcast(I32), w_words[0].bitcast(I32))
         nc.sync.dma_start(w2[:].bitcast(I32), w2_words[0].rearrange("p n r -> p (n r)").bitcast(I32))
+        nc.sync.dma_start(w1[:].bitcast(I32), w_words[0].bitcast(I32))
         for plane, rows in ((w1_scale, w_scales), (w2_scale, w2_scales)):
             for q in range(4):
                 nc.sync.dma_start(plane[32 * q : 32 * q + 4, :].bitcast(I32), rows[0, 4 * q : 4 * q + 4, :].bitcast(I32))
@@ -61,8 +60,11 @@ def tile_list_signedhalves_kernel(tc, ca, sa, sb, w_words, w_scales, w2_words, w
         picked = [sbuf.tile([P, J], U8, name=f"picked{t}") for t in range(PACK)]
         level = [sbuf.tile([P, J], F32, name=f"level{t}") for t in range(PACK)]
         for t in range(PACK):
-            nc.vector.tensor_copy(picked[t][:], table[t][:].indirect(offsets[:]))
-            nc.scalar.copy(level[t][:], picked[t][:].bitcast(FP8))
+            parts = 2 if t == PACK - 1 else 1
+            for s in range(parts):
+                c0, c1 = s * J // parts, (s + 1) * J // parts
+                nc.vector.tensor_copy(picked[t][:, c0:c1], table[t][:].indirect(offsets[:, c0 // 16 : c1 // 16]))
+                nc.scalar.copy(level[t][:, c0:c1], picked[t][:, c0:c1].bitcast(FP8))
 
         rows = [sbuf.tile([P, PACK, J], BF16, name=f"rows{z}") for z in range(2)]
         woven = [[sbuf.tile([P, HALF, PACK], BF16, name=f"woven{z}{s}", align_bytes=64) for s in range(2)] for z in range(2)]
@@ -97,26 +99,33 @@ def tile_list_signedhalves_kernel(tc, ca, sa, sb, w_words, w_scales, w2_words, w
                     stop=(z == 1),
                 )
 
-        for t in range(PACK):
-            nc.vector.tensor_scalar(rows[0][:, t, :], level[t][:], 0.0, rise[:, t : t + 1], ALU.max, ALU.mult)
+        def halves(z, t, c0, c1):
+            if z == 0:
+                nc.vector.tensor_scalar(rows[0][:, t, c0:c1], level[t][:, c0:c1], 0.0, rise[:, t : t + 1], ALU.max, ALU.mult)
+            else:
+                nc.vector.tensor_scalar(rows[1][:, t, c0:c1], level[t][:, c0:c1], 0.0, neg_fall[:, t : t + 1], ALU.min, ALU.mult)
+
+        for t in range(PACK - 1):
+            halves(0, t, 0, J)
+        halves(0, 3, 0, HALF)
         weave(nc.scalar.copy, 0, 0, 0, HALF)
-        weave(nc.scalar.copy, 0, 1, 0, HALF)
+        halves(0, 3, HALF, J)
         for t in range(PACK):
-            nc.vector.tensor_scalar(rows[1][:, t, :], level[t][:], 0.0, neg_fall[:, t : t + 1], ALU.min, ALU.mult)
+            halves(1, t, 0, J)
+        weave(nc.scalar.copy, 1, 0, 0, HALF)
+        weave(nc.vector.tensor_copy, 0, 1, 0, HALF)
         quantize(0, 0)
         multiply(0, 0)
-        weave(nc.vector.tensor_copy, 1, 0, 0, HALF)
-        weave(nc.vector.tensor_copy, 1, 1, 0, HALF - SHARE)
-        weave(nc.scalar.copy, 1, 1, HALF - SHARE, HALF)
-        quantize(1, 0)
-        multiply(1, 0)
         quantize(0, 1)
         multiply(0, 1)
+        weave(nc.vector.tensor_copy, 1, 1, 0, HALF)
+        quantize(1, 0)
+        multiply(1, 0)
         quantize(1, 1)
         multiply(1, 1)
         out_h = out.rearrange("(h p) j -> p h j", h=2)
-        for h in range(2):
-            nc.scalar.copy(first[:, h, :], acc[0][h][:])
+        nc.scalar.copy(first[:, 0, :], acc[0][0][:])
+        nc.vector.tensor_copy(first[:, 1, :], acc[0][1][:])
         nc.sync.dma_start(out_h[:, :, 0:HALF], first[:])
         nc.scalar.copy(last[0][:], acc[1][0][:])
         nc.scalar.dma_start(out[0:P, HALF:J], last[0][:])

@@ -52,21 +52,26 @@ def tile_list_signedhalves_kernel(tc, ca, sa, sb, w_words, w_scales, w2_words, w
         nc.sync.dma_start(fall[:], sb.rearrange("(p t) o -> p (t o)", t=PACK))
         nc.sync.dma_start(w2[:].bitcast(I32), w2_words[0].rearrange("p n r -> p (n r)").bitcast(I32))
         nc.sync.dma_start(w1[:].bitcast(I32), w_words[0].bitcast(I32))
-        for plane, rows in ((w1_scale, w_scales), (w2_scale, w2_scales)):
+        for plane, src in ((w1_scale, w_scales), (w2_scale, w2_scales)):
             for q in range(4):
-                nc.sync.dma_start(plane[32 * q : 32 * q + 4, :].bitcast(I32), rows[0, 4 * q : 4 * q + 4, :].bitcast(I32))
+                nc.sync.dma_start(plane[32 * q : 32 * q + 4, :].bitcast(I32), src[0, 4 * q : 4 * q + 4, :].bitcast(I32))
         nc.scalar.activation(neg_fall[:], fall[:], ACT.Copy, scale=-1.0)
 
         picked = [sbuf.tile([P, J], U8, name=f"picked{t}") for t in range(PACK)]
         level = [sbuf.tile([P, J], F32, name=f"level{t}") for t in range(PACK)]
+        rows = [sbuf.tile([P, PACK, J], BF16, name=f"rows{z}") for z in range(2)]
+        above = sbuf.tile([P, J], F32, name="above")
         for t in range(PACK):
             parts = 2 if t == PACK - 1 else 1
             for s in range(parts):
                 c0, c1 = s * J // parts, (s + 1) * J // parts
                 nc.vector.tensor_copy(picked[t][:, c0:c1], table[t][:].indirect(offsets[:, c0 // 16 : c1 // 16]))
                 nc.scalar.copy(level[t][:, c0:c1], picked[t][:, c0:c1].bitcast(FP8))
+                if t == 1:
+                    nc.scalar.activation(above[:], level[0][:], ACT.Relu)
+                if t == PACK - 1 and s == 0:
+                    nc.scalar.activation(rows[0][:, 0, :], above[:], ACT.Copy, scale=rise[:, 0:1])
 
-        rows = [sbuf.tile([P, PACK, J], BF16, name=f"rows{z}") for z in range(2)]
         woven = [[sbuf.tile([P, HALF, PACK], BF16, name=f"woven{z}{s}", align_bytes=64) for s in range(2)] for z in range(2)]
         codes = [[sbuf.tile([P, HALF], U32, name=f"codes{z}{s}", align_bytes=64) for s in range(2)] for z in range(2)]
         scales = [[sbuf.tile([P, HALF], U8, name=f"scales{z}{s}", align_bytes=64) for s in range(2)] for z in range(2)]
@@ -105,7 +110,7 @@ def tile_list_signedhalves_kernel(tc, ca, sa, sb, w_words, w_scales, w2_words, w
             else:
                 nc.vector.tensor_scalar(rows[1][:, t, c0:c1], level[t][:, c0:c1], 0.0, neg_fall[:, t : t + 1], ALU.min, ALU.mult)
 
-        for t in range(PACK - 1):
+        for t in range(1, PACK - 1):
             halves(0, t, 0, J)
         halves(0, 3, 0, HALF)
         weave(nc.scalar.copy, 0, 0, 0, HALF)

@@ -20,8 +20,12 @@ ACT = mybir.ActivationFunctionType
 
 P = 128
 PACK = 4
-HALF = J // 2
+LAST = PACK - 1
+PART = J // 2
+PER_COLUMN = 16
+QUADRANT = 32
 RUN = 4
+Z1, Z2 = 0, 1
 
 
 def tile_list_signedhalves_kernel(tc, ca, sa, sb, w_words, w_scales, w2_words, w2_scales, offs, out):
@@ -30,7 +34,7 @@ def tile_list_signedhalves_kernel(tc, ca, sa, sb, w_words, w_scales, w2_words, w
         sbuf = ctx.enter_context(tc.tile_pool(name="sbuf", bufs=1))
         psum = ctx.enter_context(tc.psum_pool(name="psum", bufs=1))
 
-        offsets = sbuf.tile([P, J // 16], U16, name="offsets")
+        offsets = sbuf.tile([P, J // PER_COLUMN], U16, name="offsets")
         table = [sbuf.tile([P, V], U8, name=f"table{t}") for t in range(PACK)]
         w1 = sbuf.tile([P, 2 * N], U8, name="w1", align_bytes=64)
         w2 = sbuf.tile([P, 4 * N], U8, name="w2", align_bytes=64)
@@ -52,87 +56,84 @@ def tile_list_signedhalves_kernel(tc, ca, sa, sb, w_words, w_scales, w2_words, w
         nc.sync.dma_start(fall[:], sb.rearrange("(p t) o -> p (t o)", t=PACK))
         nc.sync.dma_start(w2[:].bitcast(I32), w2_words[0].rearrange("p n r -> p (n r)").bitcast(I32))
         nc.sync.dma_start(w1[:].bitcast(I32), w_words[0].bitcast(I32))
-        for plane, src in ((w1_scale, w_scales), (w2_scale, w2_scales)):
-            for q in range(4):
-                nc.sync.dma_start(plane[32 * q : 32 * q + 4, :].bitcast(I32), src[0, 4 * q : 4 * q + 4, :].bitcast(I32))
+        for scale_tile, scale_rows in ((w1_scale, w_scales), (w2_scale, w2_scales)):
+            for q in range(P // QUADRANT):
+                nc.sync.dma_start(
+                    scale_tile[QUADRANT * q : QUADRANT * q + 4, :].bitcast(I32),
+                    scale_rows[0, 4 * q : 4 * q + 4, :].bitcast(I32),
+                )
         nc.scalar.activation(neg_fall[:], fall[:], ACT.Copy, scale=-1.0)
 
         picked = [sbuf.tile([P, J], U8, name=f"picked{t}") for t in range(PACK)]
         level = [sbuf.tile([P, J], F32, name=f"level{t}") for t in range(PACK)]
-        rows = [sbuf.tile([P, PACK, J], BF16, name=f"rows{z}") for z in range(2)]
+        rows = [sbuf.tile([P, PACK, J], BF16, name=f"rows{z}") for z in (Z1, Z2)]
         above = sbuf.tile([P, J], F32, name="above")
-        for t in range(PACK):
-            parts = 2 if t == PACK - 1 else 1
-            for s in range(parts):
-                c0, c1 = s * J // parts, (s + 1) * J // parts
-                nc.vector.tensor_copy(picked[t][:, c0:c1], table[t][:].indirect(offsets[:, c0 // 16 : c1 // 16]))
-                nc.scalar.copy(level[t][:, c0:c1], picked[t][:, c0:c1].bitcast(FP8))
-                if t == 1:
-                    nc.scalar.activation(above[:], level[0][:], ACT.Relu)
-                if t == PACK - 1 and s == 0:
-                    nc.scalar.activation(rows[0][:, 0, :], above[:], ACT.Copy, scale=rise[:, 0:1])
 
-        woven = [[sbuf.tile([P, HALF, PACK], BF16, name=f"woven{z}{s}", align_bytes=64) for s in range(2)] for z in range(2)]
-        codes = [[sbuf.tile([P, HALF], U32, name=f"codes{z}{s}", align_bytes=64) for s in range(2)] for z in range(2)]
-        scales = [[sbuf.tile([P, HALF], U8, name=f"scales{z}{s}", align_bytes=64) for s in range(2)] for z in range(2)]
-        acc = [[psum.tile([P, HALF], F32, name=f"acc{s}{h}") for h in range(2)] for s in range(2)]
-        first = sbuf.tile([P, 2, HALF], F32, name="first")
-        last = [sbuf.tile([P, HALF], F32, name=f"last{h}") for h in range(2)]
+        def look_up(t, j0, j1):
+            entries = offsets[:, j0 // PER_COLUMN : j1 // PER_COLUMN]
+            nc.vector.tensor_copy(picked[t][:, j0:j1], table[t][:].indirect(entries))
+            nc.scalar.copy(level[t][:, j0:j1], picked[t][:, j0:j1].bitcast(FP8))
 
-        def weave(copy, z, s, c0, c1):
+        look_up(0, 0, J)
+        look_up(1, 0, J)
+        nc.scalar.activation(above[:], level[0][:], ACT.Relu)
+        look_up(2, 0, J)
+        look_up(LAST, 0, PART)
+        nc.scalar.activation(rows[Z1][:, 0, :], above[:], ACT.Copy, scale=rise[:, 0:1])
+        look_up(LAST, PART, J)
+
+        woven = [[sbuf.tile([P, PART, PACK], BF16, name=f"woven{z}{s}", align_bytes=64) for s in range(2)] for z in (Z1, Z2)]
+        codes = [[sbuf.tile([P, PART], U32, name=f"codes{z}{s}", align_bytes=64) for s in range(2)] for z in (Z1, Z2)]
+        scales = [[sbuf.tile([P, PART], U8, name=f"scales{z}{s}", align_bytes=64) for s in range(2)] for z in (Z1, Z2)]
+        acc = [[psum.tile([P, PART], F32, name=f"acc{s}{h}") for h in range(2)] for s in range(2)]
+        res = [[sbuf.tile([P, PART], F32, name=f"res{s}{h}") for h in range(2)] for s in range(2)]
+
+        def make_row(z, t, j0, j1):
+            cut, step = (ALU.max, rise) if z == Z1 else (ALU.min, neg_fall)
+            nc.vector.tensor_scalar(rows[z][:, t, j0:j1], level[t][:, j0:j1], 0.0, step[:, t : t + 1], cut, ALU.mult)
+
+        def weave(copy, z, s):
             copy(
-                woven[z][s][:, c0:c1, :].rearrange("p (c i) t -> p c t i", i=RUN),
-                rows[z][:, :, s * HALF + c0 : s * HALF + c1].rearrange("p t (c i) -> p c t i", i=RUN),
+                woven[z][s][:].rearrange("p (c i) t -> p c t i", i=RUN),
+                rows[z][:, :, s * PART : (s + 1) * PART].rearrange("p t (c i) -> p c t i", i=RUN),
             )
 
-        def quantize(z, s):
-            nc.vector.quantize_mx(codes[z][s][:].bitcast(E4M3X4), scales[z][s][:], woven[z][s][:].rearrange("p j t -> p (j t)"))
-
-        def multiply(z, s):
+        def quantize_and_multiply(z, s):
+            moving = codes[z][s][:].bitcast(E4M3X4)
+            nc.vector.quantize_mx(moving, scales[z][s][:], woven[z][s][:].rearrange("p j t -> p (j t)"))
             for h in range(2):
-                if z == 0:
-                    words, plane = w1[:, 2 * P * h : 2 * P * (h + 1)].bitcast(E2M1X4), w1_scale
+                if z == Z1:
+                    words, scale_tile = w1[:, 2 * P * h : 2 * P * (h + 1)].bitcast(E2M1X4), w1_scale
                 else:
-                    words, plane = w2[:, 4 * P * h : 4 * P * (h + 1)].bitcast(E5M2X4), w2_scale
+                    words, scale_tile = w2[:, 4 * P * h : 4 * P * (h + 1)].bitcast(E5M2X4), w2_scale
                 nc.tensor.matmul_mx(
                     acc[s][h][:],
                     lhsT=words,
-                    lhsT_scale=plane[:, P * h : P * (h + 1)],
-                    rhs=codes[z][s][:].bitcast(E4M3X4),
+                    lhsT_scale=scale_tile[:, P * h : P * (h + 1)],
+                    rhs=moving,
                     rhs_scale=scales[z][s][:],
-                    start=(z == 0),
-                    stop=(z == 1),
+                    start=(z == Z1),
+                    stop=(z == Z2),
                 )
 
-        def halves(z, t, c0, c1):
-            if z == 0:
-                nc.vector.tensor_scalar(rows[0][:, t, c0:c1], level[t][:, c0:c1], 0.0, rise[:, t : t + 1], ALU.max, ALU.mult)
-            else:
-                nc.vector.tensor_scalar(rows[1][:, t, c0:c1], level[t][:, c0:c1], 0.0, neg_fall[:, t : t + 1], ALU.min, ALU.mult)
-
-        for t in range(1, PACK - 1):
-            halves(0, t, 0, J)
-        halves(0, 3, 0, HALF)
-        weave(nc.scalar.copy, 0, 0, 0, HALF)
-        halves(0, 3, HALF, J)
+        for t in range(1, LAST):
+            make_row(Z1, t, 0, J)
+        make_row(Z1, LAST, 0, PART)
+        weave(nc.scalar.copy, Z1, 0)
+        make_row(Z1, LAST, PART, J)
         for t in range(PACK):
-            halves(1, t, 0, J)
-        weave(nc.scalar.copy, 1, 0, 0, HALF)
-        weave(nc.vector.tensor_copy, 0, 1, 0, HALF)
-        quantize(0, 0)
-        multiply(0, 0)
-        quantize(0, 1)
-        multiply(0, 1)
-        weave(nc.vector.tensor_copy, 1, 1, 0, HALF)
-        quantize(1, 0)
-        multiply(1, 0)
-        quantize(1, 1)
-        multiply(1, 1)
-        out_h = out.rearrange("(h p) j -> p h j", h=2)
-        nc.scalar.copy(first[:, 0, :], acc[0][0][:])
-        nc.vector.tensor_copy(first[:, 1, :], acc[0][1][:])
-        nc.sync.dma_start(out_h[:, :, 0:HALF], first[:])
-        nc.scalar.copy(last[0][:], acc[1][0][:])
-        nc.scalar.dma_start(out[0:P, HALF:J], last[0][:])
-        nc.vector.tensor_copy(last[1][:], acc[1][1][:])
-        nc.sync.dma_start(out[P : 2 * P, HALF:J], last[1][:])
+            make_row(Z2, t, 0, J)
+        weave(nc.scalar.copy, Z2, 0)
+        weave(nc.vector.tensor_copy, Z1, 1)
+        quantize_and_multiply(Z1, 0)
+        quantize_and_multiply(Z1, 1)
+        weave(nc.vector.tensor_copy, Z2, 1)
+        quantize_and_multiply(Z2, 0)
+        quantize_and_multiply(Z2, 1)
+
+        for s in range(2):
+            cases = slice(s * PART, (s + 1) * PART)
+            nc.scalar.copy(res[s][0][:], acc[s][0][:])
+            nc.scalar.dma_start(out[0:P, cases], res[s][0][:])
+            nc.vector.tensor_copy(res[s][1][:], acc[s][1][:])
+            nc.sync.dma_start(out[P : 2 * P, cases], res[s][1][:])

from contextlib import ExitStack

import concourse.mybir as mybir

K, V, J, N = 512, 1024, 256, 256
FLOPS = 2 * 2 * K * N * J

F32 = mybir.dt.float32
BF16 = mybir.dt.bfloat16
I32 = mybir.dt.int32
U32 = mybir.dt.uint32
U16 = mybir.dt.uint16
U8 = mybir.dt.uint8
FP8 = mybir.dt.float8_e4m3fn
E4M3X4 = mybir.dt.float8_e4m3fn_x4
E5M2X4 = mybir.dt.float8_e5m2_x4
E2M1X4 = mybir.dt.float4_e2m1fn_x4
ALU = mybir.AluOpType
ACT = mybir.ActivationFunctionType

P = 128
PACK = 4
LAST = PACK - 1
PART = J // 2
PER_COLUMN = 16
QUADRANT = 32
RUN = 4
Z1, Z2 = 0, 1


def tile_list_signedhalves_kernel(tc, ca, sa, sb, w_words, w_scales, w2_words, w2_scales, offs, out):
    nc = tc.nc
    with ExitStack() as ctx:
        sbuf = ctx.enter_context(tc.tile_pool(name="sbuf", bufs=1))
        psum = ctx.enter_context(tc.psum_pool(name="psum", bufs=1))

        offsets = sbuf.tile([P, J // PER_COLUMN], U16, name="offsets")
        table = [sbuf.tile([P, V], U8, name=f"table{t}") for t in range(PACK)]
        w1 = sbuf.tile([P, 2 * N], U8, name="w1", align_bytes=64)
        w2 = sbuf.tile([P, 4 * N], U8, name="w2", align_bytes=64)
        w1_scale = sbuf.tile([P, N], U8, name="w1_scale", align_bytes=64)
        w2_scale = sbuf.tile([P, N], U8, name="w2_scale", align_bytes=64)
        rise = sbuf.tile([P, PACK], F32, name="rise")
        fall = sbuf.tile([P, PACK], F32, name="fall")
        neg_fall = sbuf.tile([P, PACK], F32, name="neg_fall")

        nc.vector.memset(w1_scale[:].bitcast(I32), 0)
        nc.vector.memset(w2_scale[:].bitcast(I32), 0)

        ca_rows = ca.rearrange("(p t) v -> t p v", t=PACK)
        nc.sync.dma_start(table[0][:], ca_rows[0])
        nc.sync.dma_start(offsets[:], offs)
        for t in range(1, PACK):
            nc.sync.dma_start(table[t][:], ca_rows[t])
        nc.sync.dma_start(rise[:], sa.rearrange("(p t) o -> p (t o)", t=PACK))
        nc.sync.dma_start(fall[:], sb.rearrange("(p t) o -> p (t o)", t=PACK))
        nc.sync.dma_start(w2[:].bitcast(I32), w2_words[0].rearrange("p n r -> p (n r)").bitcast(I32))
        nc.sync.dma_start(w1[:].bitcast(I32), w_words[0].bitcast(I32))
        for scale_tile, scale_rows in ((w1_scale, w_scales), (w2_scale, w2_scales)):
            for q in range(P // QUADRANT):
                nc.sync.dma_start(
                    scale_tile[QUADRANT * q : QUADRANT * q + 4, :].bitcast(I32),
                    scale_rows[0, 4 * q : 4 * q + 4, :].bitcast(I32),
                )
        nc.scalar.activation(neg_fall[:], fall[:], ACT.Copy, scale=-1.0)

        picked = [sbuf.tile([P, J], U8, name=f"picked{t}") for t in range(PACK)]
        level = [sbuf.tile([P, J], F32, name=f"level{t}") for t in range(PACK)]
        rows = [sbuf.tile([P, PACK, J], BF16, name=f"rows{z}") for z in (Z1, Z2)]
        above = sbuf.tile([P, J], F32, name="above")

        def look_up(t, j0, j1):
            entries = offsets[:, j0 // PER_COLUMN : j1 // PER_COLUMN]
            nc.vector.tensor_copy(picked[t][:, j0:j1], table[t][:].indirect(entries))
            nc.scalar.copy(level[t][:, j0:j1], picked[t][:, j0:j1].bitcast(FP8))

        look_up(0, 0, J)
        look_up(1, 0, J)
        nc.scalar.activation(above[:], level[0][:], ACT.Relu)
        look_up(2, 0, J)
        look_up(LAST, 0, PART)
        nc.scalar.activation(rows[Z1][:, 0, :], above[:], ACT.Copy, scale=rise[:, 0:1])
        look_up(LAST, PART, J)

        woven = [[sbuf.tile([P, PART, PACK], BF16, name=f"woven{z}{s}", align_bytes=64) for s in range(2)] for z in (Z1, Z2)]
        codes = [[sbuf.tile([P, PART], U32, name=f"codes{z}{s}", align_bytes=64) for s in range(2)] for z in (Z1, Z2)]
        scales = [[sbuf.tile([P, PART], U8, name=f"scales{z}{s}", align_bytes=64) for s in range(2)] for z in (Z1, Z2)]
        acc = [[psum.tile([P, PART], F32, name=f"acc{s}{h}") for h in range(2)] for s in range(2)]
        res = [[sbuf.tile([P, PART], F32, name=f"res{s}{h}") for h in range(2)] for s in range(2)]

        def make_row(z, t, j0, j1):
            cut, step = (ALU.max, rise) if z == Z1 else (ALU.min, neg_fall)
            nc.vector.tensor_scalar(rows[z][:, t, j0:j1], level[t][:, j0:j1], 0.0, step[:, t : t + 1], cut, ALU.mult)

        def weave(copy, z, s):
            copy(
                woven[z][s][:].rearrange("p (c i) t -> p c t i", i=RUN),
                rows[z][:, :, s * PART : (s + 1) * PART].rearrange("p t (c i) -> p c t i", i=RUN),
            )

        def quantize_and_multiply(z, s):
            moving = codes[z][s][:].bitcast(E4M3X4)
            nc.vector.quantize_mx(moving, scales[z][s][:], woven[z][s][:].rearrange("p j t -> p (j t)"))
            for h in range(2):
                if z == Z1:
                    words, scale_tile = w1[:, 2 * P * h : 2 * P * (h + 1)].bitcast(E2M1X4), w1_scale
                else:
                    words, scale_tile = w2[:, 4 * P * h : 4 * P * (h + 1)].bitcast(E5M2X4), w2_scale
                nc.tensor.matmul_mx(
                    acc[s][h][:],
                    lhsT=words,
                    lhsT_scale=scale_tile[:, P * h : P * (h + 1)],
                    rhs=moving,
                    rhs_scale=scales[z][s][:],
                    start=(z == Z1),
                    stop=(z == Z2),
                )

        for t in range(1, LAST):
            make_row(Z1, t, 0, J)
        make_row(Z1, LAST, 0, PART)
        weave(nc.scalar.copy, Z1, 0)
        make_row(Z1, LAST, PART, J)
        for t in range(PACK):
            make_row(Z2, t, 0, J)
        weave(nc.scalar.copy, Z2, 0)
        weave(nc.vector.tensor_copy, Z1, 1)
        quantize_and_multiply(Z1, 0)
        quantize_and_multiply(Z1, 1)
        weave(nc.vector.tensor_copy, Z2, 1)
        quantize_and_multiply(Z2, 0)
        quantize_and_multiply(Z2, 1)

        for s in range(2):
            cases = slice(s * PART, (s + 1) * PART)
            nc.scalar.copy(res[s][0][:], acc[s][0][:])
            nc.scalar.dma_start(out[0:P, cases], res[s][0][:])
            nc.vector.tensor_copy(res[s][1][:], acc[s][1][:])
            nc.sync.dma_start(out[P : 2 * P, cases], res[s][1][:])
